import numpy as np, ml_dtypes
CORES = [7,391,135,263,15,399,143,271]
N = 8
W, KW = 64, 7
H = KW // 2
def setup_inputs(rng):
    return {"x": rng.standard_normal((N, 128, W), dtype=np.float32).astype(ml_dtypes.bfloat16), "t": rng.standard_normal((N, 128, KW * W), dtype=np.float32).astype(ml_dtypes.bfloat16)}
def setup_inputs_big(rng):
    d = setup_inputs(rng)
    for k in ("x", "t"): d[k] = (d[k].astype(np.float32) * 1024.0).astype(d[k].dtype)
    return d
def setup_inputs_small(rng):
    d = setup_inputs(rng)
    for k in ("x", "t"): d[k] = (d[k].astype(np.float32) * (1 / 1024.0)).astype(d[k].dtype)
    return d
def reference(x, t):
    X, T = x.astype(np.float64), t.astype(np.float64)
    g = np.concatenate(list(X), axis=1)
    p = np.concatenate([g[:, -H:], g, g[:, :H]], axis=1)
    y = np.stack([sum(T[r][:, W * i:W * i + W] * p[:, W * r + i:W * r + i + W] for i in range(KW)) for r in range(N)])
    return {"y": y.astype(ml_dtypes.bfloat16 if x.dtype != np.float64 else np.float64)}

@@ -1,0 +1,132 @@
+from concourse.mybir import AluOpType
+
+W, KW = 64, 7
+H = KW // 2
+NB = H + 1
+
+SCRATCH = {
+    "stage": ("dram", [128, H], "bfloat16"),
+    "passon": ("dram", [128, H], "bfloat16"),
+    "xs": ("sbuf", [128, W], "bfloat16"),
+    "ts": ("sbuf", [128, KW * W], "bfloat16"),
+    "hl": ("sbuf", [128, H], "bfloat16"),
+    "hr": ("sbuf", [128, H], "bfloat16"),
+    "prod": ("sbuf", [128, KW * W], "float32"),
+    "s3": ("sbuf", [128, 3 * W], "float32"),
+    "ab": ("sbuf", [128, 2 * W], "float32"),
+    "ql": ("sbuf", [128, NB * H], "float32"),
+    "qr": ("sbuf", [128, NB * H], "float32"),
+    "sl": ("sbuf", [128, 2 * H], "float32"),
+    "sr": ("sbuf", [128, 2 * H], "float32"),
+    "yb": ("sbuf", [128, W], "bfloat16"),
+}
+SEMAPHORES = ["far", "xin", "tin", "relay", "early", "late", "sent", "vec", "stored"]
+
+
+def _engines(mask, n):
+    out, bit, k = 0, 1, 0
+    while k < n:
+        if mask & bit:
+            out |= bit
+            k += 1
+        bit <<= 1
+    return out
+
+
+def _count(mask):
+    return bin(mask).count("1")
+
+
+def rank_program(g, core, T, topo):
+    rank = T.rank_of(core)
+    if rank is None:
+        return
+    n = len(T.cores)
+    S = T.sem
+    mult, add = AluOpType.mult, AluOpType.add
+
+    sides = [d for d in (-1, 1) if topo.may_write(core, T.cores[(rank + d) % n])]
+    assert len(sides) == 1
+    s = sides[0]
+    partner = T.cores[(rank + s) % n]
+    beyond = T.cores[(rank + 2 * s) % n]
+    assert topo.may_write(partner, core) and topo.may_write(core, beyond)
+    left_edge, right_edge = slice(0, H), slice(W - H, W)
+    near_cols, far_cols = (right_edge, left_edge) if s == 1 else (left_edge, right_edge)
+    toward = T.hl if s == 1 else T.hr
+    m_partner, m_beyond = topo.mask(core, partner), topo.mask(core, beyond)
+    one = _engines(m_partner, 1)
+    wide_p, wide_b = m_partner, m_beyond
+    assert 128 % _count(wide_p) == 0 and 128 % _count(wide_b) == 0
+
+    g.sync.dma_start(T.stage[:, :], T.x[:, far_cols]).then_inc(S.far, 16)
+    g.sync.dma_start(T.xs[:, :], T.x[:, :]).then_inc(S.xin, 16)
+    g.sync.dma_start(T.ts[:, :], T.t[:, :]).then_inc(S.tin, 16)
+
+    rid, pid = topo.addr(partner, core)
+    g.wait_ge(S.far, 16)
+    g.remote_dma(out_ap=T.passon[:, :], in_ap=T.stage[:, :], remote_sem=S.relay, local_sem=S.sent,
+                 pid=pid, routing_id=rid, dma_engine_mask=one)
+    g.wait_ge(S.xin, 16)
+    g.remote_dma(out_ap=toward[:, :], in_ap=T.xs[:, near_cols], remote_sem=S.early, local_sem=S.sent,
+                 pid=pid, routing_id=rid, dma_engine_mask=wide_p)
+    rid2, pid2 = topo.addr(beyond, core)
+    g.wait_ge(S.relay, _count(one))
+    g.remote_dma(out_ap=toward[:, :], in_ap=T.passon[:, :], remote_sem=S.late, local_sem=S.sent,
+                 pid=pid2, routing_id=rid2, dma_engine_mask=wide_b)
+    g.wait_ge(S.sent, _count(one) + _count(wide_p) + _count(wide_b))
+
+    v = g.vector
+    done = [0]
+
+    def op(instr):
+        instr.then_inc(S.vec, 1)
+        done[0] += 1
+
+    def settle():
+        v.wait_ge(S.vec, done[0])
+
+    op(v.memset(T.prod[:, :], 0.0))
+    op(v.memset(T.ql[:, :], 0.0))
+    op(v.memset(T.qr[:, :], 0.0))
+    settle()
+    v.wait_ge(S.xin, 16)
+    v.wait_ge(S.tin, 16)
+    for i in range(KW):
+        lo, hi = max(0, H - i), min(W, W + H - i)
+        op(v.tensor_tensor(out=T.prod[:, W * i + lo:W * i + hi], in0=T.ts[:, W * i + lo:W * i + hi],
+                           in1=T.xs[:, lo + i - H:hi + i - H], op=mult))
+    settle()
+    op(v.tensor_tensor(out=T.s3[:, :], in0=T.prod[:, 0:3 * W], in1=T.prod[:, 3 * W:6 * W], op=add))
+    settle()
+    op(v.tensor_tensor(out=T.ab[:, 0:W], in0=T.s3[:, 0:W], in1=T.s3[:, W:2 * W], op=add))
+    op(v.tensor_tensor(out=T.ab[:, W:2 * W], in0=T.s3[:, 2 * W:3 * W], in1=T.prod[:, 6 * W:7 * W], op=add))
+    settle()
+    op(v.tensor_tensor(out=T.yb[:, H:W - H], in0=T.ab[:, H:W - H], in1=T.ab[:, W + H:2 * W - H], op=add))
+    op(v.tensor_tensor(out=T.ql[:, H * H:NB * H], in0=T.ab[:, 0:H], in1=T.ab[:, W:W + H], op=add))
+    op(v.tensor_tensor(out=T.qr[:, H * H:NB * H], in0=T.ab[:, W - H:W], in1=T.ab[:, 2 * W - H:2 * W], op=add))
+
+    def finish(left):
+        for j in range(H):
+            if left:
+                op(v.tensor_tensor(out=T.ql[:, j * H:j * H + H - j], in0=T.ts[:, W * j:W * j + H - j],
+                                   in1=T.hl[:, j:H], op=mult))
+            else:
+                i = KW - 1 - j
+                op(v.tensor_tensor(out=T.qr[:, j * H + j:(j + 1) * H], in0=T.ts[:, W * i + W - H + j:W * i + W],
+                                   in1=T.hr[:, 0:H - j], op=mult))
+        q, h2, cols = (T.ql, T.sl, left_edge) if left else (T.qr, T.sr, right_edge)
+        settle()
+        op(v.tensor_tensor(out=h2[:, :], in0=q[:, 0:2 * H], in1=q[:, 2 * H:4 * H], op=add))
+        settle()
+        op(v.tensor_tensor(out=T.yb[:, cols], in0=h2[:, 0:H], in1=h2[:, H:2 * H], op=add))
+
+    v.wait_ge(S.early, _count(topo.mask(partner, core)))
+    finish(left=(s == -1))
+    behind = T.cores[(rank - 2 * s) % n]
+    v.wait_ge(S.late, _count(topo.mask(behind, core)))
+    finish(left=(s == 1))
+
+    g.scalar.wait_ge(S.vec, done[0])
+    g.scalar.dma_start(T.y[:, :], T.yb[:, :]).then_inc(S.stored, 16)
+    g.scalar.wait_ge(S.stored, 16)

@@ -1,8 +1,7 @@
-from concourse.mybir import AluOpType
+from concourse.mybir import AluOpType, ActivationFunctionType
 
 W, KW = 64, 7
 H = KW // 2
-NB = H + 1
 
 SCRATCH = {
     "stage": ("dram", [128, H], "bfloat16"),
@@ -14,13 +13,21 @@ SCRATCH = {
     "prod": ("sbuf", [128, KW * W], "float32"),
     "s3": ("sbuf", [128, 3 * W], "float32"),
     "ab": ("sbuf", [128, 2 * W], "float32"),
-    "ql": ("sbuf", [128, NB * H], "float32"),
-    "qr": ("sbuf", [128, NB * H], "float32"),
-    "sl": ("sbuf", [128, 2 * H], "float32"),
-    "sr": ("sbuf", [128, 2 * H], "float32"),
+    "ll": ("sbuf", [128, H], "float32"),
+    "lr": ("sbuf", [128, H], "float32"),
+    "tal": ("sbuf", [128, 2], "bfloat16"),
+    "tar": ("sbuf", [128, 2], "bfloat16"),
+    "tfl": ("sbuf", [128, 4], "float32"),
+    "tfr": ("sbuf", [128, 4], "float32"),
+    "pql": ("sbuf", [128, 2], "float32"),
+    "pqr": ("sbuf", [128, 2], "float32"),
+    "ul": ("sbuf", [128, 1], "float32"),
+    "ur": ("sbuf", [128, 1], "float32"),
+    "wl": ("sbuf", [128, 1], "float32"),
+    "wr": ("sbuf", [128, 1], "float32"),
     "yb": ("sbuf", [128, W], "bfloat16"),
 }
-SEMAPHORES = ["far", "xin", "tin", "relay", "early", "late", "sent", "vec", "stored"]
+SEMAPHORES = ["far", "xin", "tin", "relay", "early", "late", "sent", "vec", "loc", "prep", "act", "stored"]
 
 
 def _engines(mask, n):
@@ -37,6 +44,10 @@ def _count(mask):
     return bin(mask).count("1")
 
 
+def _col(ap, c):
+    return ap[:, c:c + 1]
+
+
 def rank_program(g, core, T, topo):
     rank = T.rank_of(core)
     if rank is None:
@@ -44,6 +55,7 @@ def rank_program(g, core, T, topo):
     n = len(T.cores)
     S = T.sem
     mult, add = AluOpType.mult, AluOpType.add
+    ident, copy = ActivationFunctionType.Identity, ActivationFunctionType.Copy
 
     sides = [d for d in (-1, 1) if topo.may_write(core, T.cores[(rank + d) % n])]
     assert len(sides) == 1
@@ -76,6 +88,29 @@ def rank_program(g, core, T, topo):
                  pid=pid2, routing_id=rid2, dma_engine_mask=wide_b)
     g.wait_ge(S.sent, _count(one) + _count(wide_p) + _count(wide_b))
 
+    def plan(left):
+        if left:
+            tab = lambda c, k: W * (k - c) + c
+            return dict(halo=T.hl, L=T.ll, ta=T.tal, tf=T.tfl, pq=T.pql, u=T.ul, w=T.wl, base=0,
+                        c3=0, k3=(0, 1, 2), c2=1, k2=(1, 2), c1=2, k1=2, tab=tab)
+        tab = lambda c, k: W * (W + H + k - c) + c
+        return dict(halo=T.hr, L=T.lr, ta=T.tar, tf=T.tfr, pq=T.pqr, u=T.ur, w=T.wr, base=W - H,
+                    c3=W - 1, k3=(0, 1, 2), c2=W - 2, k2=(0, 1), c1=W - H, k1=0, tab=tab)
+
+    P = {True: plan(True), False: plan(False)}
+
+    a = g.scalar
+    a.wait_ge(S.tin, 16)
+    nprep = 0
+    for left in (True, False):
+        p = P[left]
+        for j in (0, 1):
+            a.activation(_col(p["ta"], j), _col(T.ts, p["tab"](p["c3"], p["k3"][1 + j])), copy).then_inc(S.prep, 1)
+            a.activation(_col(p["tf"], j), _col(T.ts, p["tab"](p["c2"], p["k2"][j])), copy).then_inc(S.prep, 1)
+        a.activation(_col(p["tf"], 2), _col(T.ts, p["tab"](p["c1"], p["k1"])), copy).then_inc(S.prep, 1)
+        a.activation(_col(p["tf"], 3), _col(T.ts, p["tab"](p["c3"], p["k3"][0])), copy).then_inc(S.prep, 1)
+        nprep += 6
+
     v = g.vector
     done = [0]
 
@@ -87,8 +122,6 @@ def rank_program(g, core, T, topo):
         v.wait_ge(S.vec, done[0])
 
     op(v.memset(T.prod[:, :], 0.0))
-    op(v.memset(T.ql[:, :], 0.0))
-    op(v.memset(T.qr[:, :], 0.0))
     settle()
     v.wait_ge(S.xin, 16)
     v.wait_ge(S.tin, 16)
@@ -102,31 +135,43 @@ def rank_program(g, core, T, topo):
     op(v.tensor_tensor(out=T.ab[:, 0:W], in0=T.s3[:, 0:W], in1=T.s3[:, W:2 * W], op=add))
     op(v.tensor_tensor(out=T.ab[:, W:2 * W], in0=T.s3[:, 2 * W:3 * W], in1=T.prod[:, 6 * W:7 * W], op=add))
     settle()
+    v.tensor_tensor(out=T.ll[:, :], in0=T.ab[:, 0:H], in1=T.ab[:, W:W + H], op=add).then_inc(S.loc, 1)
+    v.tensor_tensor(out=T.lr[:, :], in0=T.ab[:, W - H:W], in1=T.ab[:, 2 * W - H:2 * W], op=add).then_inc(S.loc, 1)
     op(v.tensor_tensor(out=T.yb[:, H:W - H], in0=T.ab[:, H:W - H], in1=T.ab[:, W + H:2 * W - H], op=add))
-    op(v.tensor_tensor(out=T.ql[:, H * H:NB * H], in0=T.ab[:, 0:H], in1=T.ab[:, W:W + H], op=add))
-    op(v.tensor_tensor(out=T.qr[:, H * H:NB * H], in0=T.ab[:, W - H:W], in1=T.ab[:, 2 * W - H:2 * W], op=add))
+    v.wait_ge(S.loc, 2)
+    v.wait_ge(S.prep, nprep)
+    a.wait_ge(S.prep, nprep)
+    a.wait_ge(S.loc, 2)
 
-    def finish(left):
-        for j in range(H):
-            if left:
-                op(v.tensor_tensor(out=T.ql[:, j * H:j * H + H - j], in0=T.ts[:, W * j:W * j + H - j],
-                                   in1=T.hl[:, j:H], op=mult))
-            else:
-                i = KW - 1 - j
-                op(v.tensor_tensor(out=T.qr[:, j * H + j:(j + 1) * H], in0=T.ts[:, W * i + W - H + j:W * i + W],
-                                   in1=T.hr[:, 0:H - j], op=mult))
-        q, h2, cols = (T.ql, T.sl, left_edge) if left else (T.qr, T.sr, right_edge)
-        settle()
-        op(v.tensor_tensor(out=h2[:, :], in0=q[:, 0:2 * H], in1=q[:, 2 * H:4 * H], op=add))
-        settle()
-        op(v.tensor_tensor(out=T.yb[:, cols], in0=h2[:, 0:H], in1=h2[:, H:2 * H], op=add))
+    acts = [0]
 
-    v.wait_ge(S.early, _count(topo.mask(partner, core)))
-    finish(left=(s == -1))
+    def finish(left, sem, count):
+        p = P[left]
+        halo, L, base = p["halo"], p["L"], p["base"]
+        c, (k0, k1, k2) = p["c3"], p["k3"]
+        v.wait_ge(sem, count)
+        op(v.tensor_tensor(out=p["pq"][:, 0:2], in0=p["ta"][:, 0:2], in1=halo[:, k1:k2 + 1], op=mult))
+        op(v.tensor_scalar(_col(p["u"], 0), _col(halo, k0), _col(p["tf"], 3), _col(L, c - base), mult, add))
+        settle()
+        op(v.tensor_scalar(_col(T.yb, c), _col(p["u"], 0), _col(p["pq"], 0), _col(p["pq"], 1), add, add))
+        a.wait_ge(sem, count)
+        c = p["c1"]
+        a.activation(_col(T.yb, c), _col(halo, p["k1"]), ident, bias=_col(L, c - base),
+                     scale=_col(p["tf"], 2)).then_inc(S.act, 1)
+        c = p["c2"]
+        a.activation(_col(p["w"], 0), _col(halo, p["k2"][0]), ident, bias=_col(L, c - base),
+                     scale=_col(p["tf"], 0)).then_inc(S.act, 1)
+        acts[0] += 2
+        a.wait_ge(S.act, acts[0])
+        a.activation(_col(T.yb, c), _col(halo, p["k2"][1]), ident, bias=_col(p["w"], 0),
+                     scale=_col(p["tf"], 1)).then_inc(S.act, 1)
+        acts[0] += 1
+
+    finish(s == -1, S.early, _count(topo.mask(partner, core)))
     behind = T.cores[(rank - 2 * s) % n]
-    v.wait_ge(S.late, _count(topo.mask(behind, core)))
-    finish(left=(s == 1))
+    finish(s == 1, S.late, _count(topo.mask(behind, core)))
 
-    g.scalar.wait_ge(S.vec, done[0])
-    g.scalar.dma_start(T.y[:, :], T.yb[:, :]).then_inc(S.stored, 16)
-    g.scalar.wait_ge(S.stored, 16)
+    a.wait_ge(S.act, acts[0])
+    a.wait_ge(S.vec, done[0])
+    a.dma_start(T.y[:, :], T.yb[:, :]).then_inc(S.stored, 16)
+    a.wait_ge(S.stored, 16)

from concourse.mybir import AluOpType, ActivationFunctionType

W, KW = 64, 7
H = KW // 2

SCRATCH = {
    "stage": ("dram", [128, H], "bfloat16"),
    "passon": ("dram", [128, H], "bfloat16"),
    "xs": ("sbuf", [128, W], "bfloat16"),
    "ts": ("sbuf", [128, KW * W], "bfloat16"),
    "hl": ("sbuf", [128, H], "bfloat16"),
    "hr": ("sbuf", [128, H], "bfloat16"),
    "prod": ("sbuf", [128, KW * W], "float32"),
    "s3": ("sbuf", [128, 3 * W], "float32"),
    "ab": ("sbuf", [128, 2 * W], "float32"),
    "ll": ("sbuf", [128, H], "float32"),
    "lr": ("sbuf", [128, H], "float32"),
    "tal": ("sbuf", [128, 2], "bfloat16"),
    "tar": ("sbuf", [128, 2], "bfloat16"),
    "tfl": ("sbuf", [128, 4], "float32"),
    "tfr": ("sbuf", [128, 4], "float32"),
    "pql": ("sbuf", [128, 2], "float32"),
    "pqr": ("sbuf", [128, 2], "float32"),
    "ul": ("sbuf", [128, 1], "float32"),
    "ur": ("sbuf", [128, 1], "float32"),
    "wl": ("sbuf", [128, 1], "float32"),
    "wr": ("sbuf", [128, 1], "float32"),
    "yb": ("sbuf", [128, W], "bfloat16"),
}
SEMAPHORES = ["far", "xin", "tin", "relay", "early", "late", "sent", "vec", "loc", "prep", "act", "stored"]


def _engines(mask, n):
    out, bit, k = 0, 1, 0
    while k < n:
        if mask & bit:
            out |= bit
            k += 1
        bit <<= 1
    return out


def _count(mask):
    return bin(mask).count("1")


def _col(ap, c):
    return ap[:, c:c + 1]


def rank_program(g, core, T, topo):
    rank = T.rank_of(core)
    if rank is None:
        return
    n = len(T.cores)
    S = T.sem
    mult, add = AluOpType.mult, AluOpType.add
    ident, copy = ActivationFunctionType.Identity, ActivationFunctionType.Copy

    sides = [d for d in (-1, 1) if topo.may_write(core, T.cores[(rank + d) % n])]
    assert len(sides) == 1
    s = sides[0]
    partner = T.cores[(rank + s) % n]
    beyond = T.cores[(rank + 2 * s) % n]
    assert topo.may_write(partner, core) and topo.may_write(core, beyond)
    left_edge, right_edge = slice(0, H), slice(W - H, W)
    near_cols, far_cols = (right_edge, left_edge) if s == 1 else (left_edge, right_edge)
    toward = T.hl if s == 1 else T.hr
    m_partner, m_beyond = topo.mask(core, partner), topo.mask(core, beyond)
    one = _engines(m_partner, 1)
    wide_p, wide_b = m_partner, m_beyond
    assert 128 % _count(wide_p) == 0 and 128 % _count(wide_b) == 0

    g.sync.dma_start(T.stage[:, :], T.x[:, far_cols]).then_inc(S.far, 16)
    g.sync.dma_start(T.xs[:, :], T.x[:, :]).then_inc(S.xin, 16)
    g.sync.dma_start(T.ts[:, :], T.t[:, :]).then_inc(S.tin, 16)

    rid, pid = topo.addr(partner, core)
    g.wait_ge(S.far, 16)
    g.remote_dma(out_ap=T.passon[:, :], in_ap=T.stage[:, :], remote_sem=S.relay, local_sem=S.sent,
                 pid=pid, routing_id=rid, dma_engine_mask=one)
    g.wait_ge(S.xin, 16)
    g.remote_dma(out_ap=toward[:, :], in_ap=T.xs[:, near_cols], remote_sem=S.early, local_sem=S.sent,
                 pid=pid, routing_id=rid, dma_engine_mask=wide_p)
    rid2, pid2 = topo.addr(beyond, core)
    g.wait_ge(S.relay, _count(one))
    g.remote_dma(out_ap=toward[:, :], in_ap=T.passon[:, :], remote_sem=S.late, local_sem=S.sent,
                 pid=pid2, routing_id=rid2, dma_engine_mask=wide_b)
    g.wait_ge(S.sent, _count(one) + _count(wide_p) + _count(wide_b))

    def plan(left):
        if left:
            tab = lambda c, k: W * (k - c) + c
            return dict(halo=T.hl, L=T.ll, ta=T.tal, tf=T.tfl, pq=T.pql, u=T.ul, w=T.wl, base=0,
                        c3=0, k3=(0, 1, 2), c2=1, k2=(1, 2), c1=2, k1=2, tab=tab)
        tab = lambda c, k: W * (W + H + k - c) + c
        return dict(halo=T.hr, L=T.lr, ta=T.tar, tf=T.tfr, pq=T.pqr, u=T.ur, w=T.wr, base=W - H,
                    c3=W - 1, k3=(0, 1, 2), c2=W - 2, k2=(0, 1), c1=W - H, k1=0, tab=tab)

    P = {True: plan(True), False: plan(False)}

    a = g.scalar
    a.wait_ge(S.tin, 16)
    nprep = 0
    for left in (True, False):
        p = P[left]
        for j in (0, 1):
            a.activation(_col(p["ta"], j), _col(T.ts, p["tab"](p["c3"], p["k3"][1 + j])), copy).then_inc(S.prep, 1)
            a.activation(_col(p["tf"], j), _col(T.ts, p["tab"](p["c2"], p["k2"][j])), copy).then_inc(S.prep, 1)
        a.activation(_col(p["tf"], 2), _col(T.ts, p["tab"](p["c1"], p["k1"])), copy).then_inc(S.prep, 1)
        a.activation(_col(p["tf"], 3), _col(T.ts, p["tab"](p["c3"], p["k3"][0])), copy).then_inc(S.prep, 1)
        nprep += 6

    v = g.vector
    done = [0]

    def op(instr):
        instr.then_inc(S.vec, 1)
        done[0] += 1

    def settle():
        v.wait_ge(S.vec, done[0])

    op(v.memset(T.prod[:, :], 0.0))
    settle()
    v.wait_ge(S.xin, 16)
    v.wait_ge(S.tin, 16)
    for i in range(KW):
        lo, hi = max(0, H - i), min(W, W + H - i)
        op(v.tensor_tensor(out=T.prod[:, W * i + lo:W * i + hi], in0=T.ts[:, W * i + lo:W * i + hi],
                           in1=T.xs[:, lo + i - H:hi + i - H], op=mult))
    settle()
    op(v.tensor_tensor(out=T.s3[:, :], in0=T.prod[:, 0:3 * W], in1=T.prod[:, 3 * W:6 * W], op=add))
    settle()
    op(v.tensor_tensor(out=T.ab[:, 0:W], in0=T.s3[:, 0:W], in1=T.s3[:, W:2 * W], op=add))
    op(v.tensor_tensor(out=T.ab[:, W:2 * W], in0=T.s3[:, 2 * W:3 * W], in1=T.prod[:, 6 * W:7 * W], op=add))
    settle()
    v.tensor_tensor(out=T.ll[:, :], in0=T.ab[:, 0:H], in1=T.ab[:, W:W + H], op=add).then_inc(S.loc, 1)
    v.tensor_tensor(out=T.lr[:, :], in0=T.ab[:, W - H:W], in1=T.ab[:, 2 * W - H:2 * W], op=add).then_inc(S.loc, 1)
    op(v.tensor_tensor(out=T.yb[:, H:W - H], in0=T.ab[:, H:W - H], in1=T.ab[:, W + H:2 * W - H], op=add))
    v.wait_ge(S.loc, 2)
    v.wait_ge(S.prep, nprep)
    a.wait_ge(S.prep, nprep)
    a.wait_ge(S.loc, 2)

    acts = [0]

    def finish(left, sem, count):
        p = P[left]
        halo, L, base = p["halo"], p["L"], p["base"]
        c, (k0, k1, k2) = p["c3"], p["k3"]
        v.wait_ge(sem, count)
        op(v.tensor_tensor(out=p["pq"][:, 0:2], in0=p["ta"][:, 0:2], in1=halo[:, k1:k2 + 1], op=mult))
        op(v.tensor_scalar(_col(p["u"], 0), _col(halo, k0), _col(p["tf"], 3), _col(L, c - base), mult, add))
        settle()
        op(v.tensor_scalar(_col(T.yb, c), _col(p["u"], 0), _col(p["pq"], 0), _col(p["pq"], 1), add, add))
        a.wait_ge(sem, count)
        c = p["c1"]
        a.activation(_col(T.yb, c), _col(halo, p["k1"]), ident, bias=_col(L, c - base),
                     scale=_col(p["tf"], 2)).then_inc(S.act, 1)
        c = p["c2"]
        a.activation(_col(p["w"], 0), _col(halo, p["k2"][0]), ident, bias=_col(L, c - base),
                     scale=_col(p["tf"], 0)).then_inc(S.act, 1)
        acts[0] += 2
        a.wait_ge(S.act, acts[0])
        a.activation(_col(T.yb, c), _col(halo, p["k2"][1]), ident, bias=_col(p["w"], 0),
                     scale=_col(p["tf"], 1)).then_inc(S.act, 1)
        acts[0] += 1

    finish(s == -1, S.early, _count(topo.mask(partner, core)))
    behind = T.cores[(rank - 2 * s) % n]
    finish(s == 1, S.late, _count(topo.mask(behind, core)))

    a.wait_ge(S.act, acts[0])
    a.wait_ge(S.vec, done[0])
    a.dma_start(T.y[:, :], T.yb[:, :]).then_inc(S.stored, 16)
    a.wait_ge(S.stored, 16)
